import numpy as np, ml_dtypes
CORES = [0,1,2,3,4,5,6,7,8,9,10,11,12,13,14,15]
N = 16
def setup_inputs(rng):
    return {"x": rng.standard_normal((N, 128, 64), dtype=np.float32).astype(ml_dtypes.bfloat16)}
def reference(x):
    p = 128 // N
    blocks = x.reshape(N, N, p, 64)
    return {"y": np.ascontiguousarray(blocks.transpose(1, 0, 2, 3)).reshape(N, 128, 64)}

@@ -1,0 +1,48 @@
+from concourse.bass import DstId, RemoteDMATransfer
+
+SCRATCH = {
+    "send": ("dram", [16, 128, 4], "bfloat16"),
+    "land": ("dram", [16, 128, 4], "bfloat16"),
+    "relay": ("dram", [8, 128, 4], "bfloat16"),
+}
+SEMAPHORES = ["loaded", "sent", "arrived", "relayed", "stored"]
+
+
+def rank_program(g, core, T, topo):
+    r = T.rank_of(core)
+    if r is None:
+        return
+    S = T.sem
+    base = (core // 8) * 8
+    far = 8 - base
+    owner = topo.may_write(core, far)
+
+    def tr(dst_core, engine, sem, src, dst):
+        rid, pid, _se = topo.addr(dst_core)
+        return RemoteDMATransfer(dst_ids=[DstId(rid=rid, pnc=pid)], dma_engine_mask=1 << engine,
+                                 remote_sem=sem, src=src, dst=dst)
+
+    g.dma_start(T.send[:], T.x[:]).then_inc(S.loaded, 16)
+    g.dma_start(T.land[r], T.x[8 * r:8 * r + 8, :]).then_inc(S.loaded, 16)
+    g.wait_ge(S.loaded, 32)
+
+    peers = [j for j in range(base, base + 8) if j != core]
+    if owner:
+        g.remote_dma_fused([tr(far + d, d, S.arrived, T.send[far + d], T.land[r]) for d in range(8)],
+                           local_sem=S.sent)
+        g.remote_dma_fused([tr(j, 8 + i, S.arrived, T.send[j], T.land[r]) for i, j in enumerate(peers)],
+                           local_sem=S.sent)
+        g.wait_ge(S.relayed, 8)
+        g.remote_dma_fused([tr(far + d, d, S.arrived, T.relay[d], T.land[r - 2]) for d in range(8)],
+                           local_sem=S.sent)
+        nsent = 23
+    else:
+        ts = [tr(core + 2, d, S.relayed, T.send[far + d], T.relay[d]) for d in range(8)]
+        ts += [tr(j, 8 + i, S.arrived, T.send[j], T.land[r]) for i, j in enumerate(peers)]
+        g.remote_dma_fused(ts, local_sem=S.sent)
+        nsent = 15
+
+    g.wait_ge(S.arrived, 15)
+    g.dma_start(T.y[:], T.land[:]).then_inc(S.stored, 16)
+    g.wait_ge(S.sent, nsent)
+    g.wait_ge(S.stored, 16)

@@ -1,8 +1,7 @@
 from concourse.bass import DstId, RemoteDMATransfer
 
 SCRATCH = {
-    "send": ("dram", [16, 128, 4], "bfloat16"),
-    "land": ("dram", [16, 128, 4], "bfloat16"),
+    "grid": ("dram", [256, 128, 4], "bfloat16"),
     "relay": ("dram", [8, 128, 4], "bfloat16"),
 }
 SEMAPHORES = ["loaded", "sent", "arrived", "relayed", "stored"]
@@ -22,27 +21,32 @@ def rank_program(g, core, T, topo):
         return RemoteDMATransfer(dst_ids=[DstId(rid=rid, pnc=pid)], dma_engine_mask=1 << engine,
                                  remote_sem=sem, src=src, dst=dst)
 
-    g.dma_start(T.send[:], T.x[:]).then_inc(S.loaded, 16)
-    g.dma_start(T.land[r], T.x[8 * r:8 * r + 8, :]).then_inc(S.loaded, 16)
-    g.wait_ge(S.loaded, 32)
+    def mine(j):
+        return T.grid[16 * r + j]
+
+    def slot(s, j):
+        return T.grid[16 * s + j]
+
+    g.dma_start(T.grid[16 * r:16 * r + 16], T.x[:]).then_inc(S.loaded, 16)
+    g.wait_ge(S.loaded, 16)
 
     peers = [j for j in range(base, base + 8) if j != core]
     if owner:
-        g.remote_dma_fused([tr(far + d, d, S.arrived, T.send[far + d], T.land[r]) for d in range(8)],
+        g.remote_dma_fused([tr(far + d, d, S.arrived, mine(far + d), slot(r, far + d)) for d in range(8)],
                            local_sem=S.sent)
-        g.remote_dma_fused([tr(j, 8 + i, S.arrived, T.send[j], T.land[r]) for i, j in enumerate(peers)],
+        g.remote_dma_fused([tr(j, 8 + i, S.arrived, mine(j), slot(r, j)) for i, j in enumerate(peers)],
                            local_sem=S.sent)
         g.wait_ge(S.relayed, 8)
-        g.remote_dma_fused([tr(far + d, d, S.arrived, T.relay[d], T.land[r - 2]) for d in range(8)],
+        g.remote_dma_fused([tr(far + d, d, S.arrived, T.relay[d], slot(r - 2, far + d)) for d in range(8)],
                            local_sem=S.sent)
         nsent = 23
     else:
-        ts = [tr(core + 2, d, S.relayed, T.send[far + d], T.relay[d]) for d in range(8)]
-        ts += [tr(j, 8 + i, S.arrived, T.send[j], T.land[r]) for i, j in enumerate(peers)]
+        ts = [tr(core + 2, d, S.relayed, mine(far + d), T.relay[d]) for d in range(8)]
+        ts += [tr(j, 8 + i, S.arrived, mine(j), slot(r, j)) for i, j in enumerate(peers)]
         g.remote_dma_fused(ts, local_sem=S.sent)
         nsent = 15
 
     g.wait_ge(S.arrived, 15)
-    g.dma_start(T.y[:], T.land[:]).then_inc(S.stored, 16)
+    g.dma_start(T.y[:], T.grid[r::16]).then_inc(S.stored, 16)
     g.wait_ge(S.sent, nsent)
     g.wait_ge(S.stored, 16)

@@ -21,29 +21,24 @@ def rank_program(g, core, T, topo):
         return RemoteDMATransfer(dst_ids=[DstId(rid=rid, pnc=pid)], dma_engine_mask=1 << engine,
                                  remote_sem=sem, src=src, dst=dst)
 
-    def mine(j):
-        return T.grid[16 * r + j]
-
     def slot(s, j):
         return T.grid[16 * s + j]
 
     g.dma_start(T.grid[16 * r:16 * r + 16], T.x[:]).then_inc(S.loaded, 16)
     g.wait_ge(S.loaded, 16)
 
-    peers = [j for j in range(base, base + 8) if j != core]
+    near = [tr(j, 8 + i, S.arrived, slot(r, j), slot(r, j))
+            for i, j in enumerate(j for j in range(base, base + 8) if j != core)]
     if owner:
-        g.remote_dma_fused([tr(far + d, d, S.arrived, mine(far + d), slot(r, far + d)) for d in range(8)],
-                           local_sem=S.sent)
-        g.remote_dma_fused([tr(j, 8 + i, S.arrived, mine(j), slot(r, j)) for i, j in enumerate(peers)],
+        g.remote_dma_fused([tr(far + d, d, S.arrived, slot(r, far + d), slot(r, far + d)) for d in range(8)] + near,
                            local_sem=S.sent)
         g.wait_ge(S.relayed, 8)
         g.remote_dma_fused([tr(far + d, d, S.arrived, T.relay[d], slot(r - 2, far + d)) for d in range(8)],
                            local_sem=S.sent)
         nsent = 23
     else:
-        ts = [tr(core + 2, d, S.relayed, mine(far + d), T.relay[d]) for d in range(8)]
-        ts += [tr(j, 8 + i, S.arrived, mine(j), slot(r, j)) for i, j in enumerate(peers)]
-        g.remote_dma_fused(ts, local_sem=S.sent)
+        g.remote_dma_fused([tr(core + 2, d, S.relayed, slot(r, far + d), T.relay[d]) for d in range(8)] + near,
+                           local_sem=S.sent)
         nsent = 15
 
     g.wait_ge(S.arrived, 15)

from concourse.bass import DstId, RemoteDMATransfer

SCRATCH = {
    "grid": ("dram", [256, 128, 4], "bfloat16"),
    "relay": ("dram", [8, 128, 4], "bfloat16"),
}
SEMAPHORES = ["loaded", "sent", "arrived", "relayed", "stored"]


def rank_program(g, core, T, topo):
    r = T.rank_of(core)
    if r is None:
        return
    S = T.sem
    base = (core // 8) * 8
    far = 8 - base
    owner = topo.may_write(core, far)

    def tr(dst_core, engine, sem, src, dst):
        rid, pid, _se = topo.addr(dst_core)
        return RemoteDMATransfer(dst_ids=[DstId(rid=rid, pnc=pid)], dma_engine_mask=1 << engine,
                                 remote_sem=sem, src=src, dst=dst)

    def slot(s, j):
        return T.grid[16 * s + j]

    g.dma_start(T.grid[16 * r:16 * r + 16], T.x[:]).then_inc(S.loaded, 16)
    g.wait_ge(S.loaded, 16)

    near = [tr(j, 8 + i, S.arrived, slot(r, j), slot(r, j))
            for i, j in enumerate(j for j in range(base, base + 8) if j != core)]
    if owner:
        g.remote_dma_fused([tr(far + d, d, S.arrived, slot(r, far + d), slot(r, far + d)) for d in range(8)] + near,
                           local_sem=S.sent)
        g.wait_ge(S.relayed, 8)
        g.remote_dma_fused([tr(far + d, d, S.arrived, T.relay[d], slot(r - 2, far + d)) for d in range(8)],
                           local_sem=S.sent)
        nsent = 23
    else:
        g.remote_dma_fused([tr(core + 2, d, S.relayed, slot(r, far + d), T.relay[d]) for d in range(8)] + near,
                           local_sem=S.sent)
        nsent = 15

    g.wait_ge(S.arrived, 15)
    g.dma_start(T.y[:], T.grid[r::16]).then_inc(S.stored, 16)
    g.wait_ge(S.sent, nsent)
    g.wait_ge(S.stored, 16)
